import numpy as np
import ml_dtypes


def mxq(x, axis, fmt="e4m3"):
    dtype, down = {"e4m3": (ml_dtypes.float8_e4m3fn, 7), "e5m2": (ml_dtypes.float8_e5m2, 14)}[fmt]
    v = np.moveaxis(np.asarray(x, np.float32).astype(ml_dtypes.bfloat16).astype(np.float64), axis, -1)
    blocks = v.reshape(v.shape[:-1] + (-1, 32))
    amax = np.abs(blocks).max(-1, keepdims=True)
    byte = np.maximum(np.where(amax > 0, np.frexp(amax)[1] - 1 + 127, 0) - down, 1)
    scale = np.exp2(byte - 127.0)
    codes = (blocks / scale).astype(np.float32).astype(dtype).astype(np.float64)
    return np.moveaxis((codes * scale).reshape(v.shape), -1, axis)


WIDE = False


def mx_kscale(k):
    if not WIDE:
        return np.ones(k)
    levels = np.array([10, -10, 5, -5, 0])
    if k % 512:
        return np.exp2(np.random.permutation(np.resize(levels, k // 32))).repeat(32)
    a = np.empty((k // 512, 16))
    for p in range(k // 512):
        a[p, :8] = np.random.permutation(np.resize(levels, 8))
        for g in range(8):
            far = levels[np.abs(levels - a[p, g]) >= 10]
            a[p, g + 8] = far[np.random.randint(len(far))]
    return np.exp2(a.ravel()).repeat(32)


def f64(x):
    return np.asarray(x).astype(np.float64)


def striped(idx):
    return np.tile(idx.reshape(-1, 16).T, (8, 1)).astype(np.uint16)


def unstriped(offs):
    return offs[:16].T.reshape(-1).astype(np.int64)


def relu(v):
    return np.maximum(v, 0.0)


K, T, S, V, H, N = 512, 1024, 512, 256, 512, 128


def setup_inputs():
    n = np.random.standard_normal
    s = mx_kscale(K)[:, None]
    u = mx_kscale(H)
    return {
        "xT": (n((K, T)) * s).astype(np.float32),
        "w1": (n((K, H)) / np.sqrt(2 * K) / s * u).astype(np.float32),
        "w2": (n((K, H)) / np.sqrt(2 * K) / s * u).astype(np.float32),
        "w3": (n((H, N)) / np.sqrt(H) / u[:, None]).astype(np.float32),
        "offs": striped(np.random.permutation(T)[:S]),
        "cen": striped(np.random.permutation(S)[:V]),
        "pos1": striped(np.random.permutation(S)[:V]),
        "pos2": striped(np.random.permutation(S)[:V]),
        "pos3": striped(np.random.permutation(S)[:V]),
    }


def reference(xT, w1, w2, w3, offs, cen, pos1, pos2, pos3):
    xq = mxq(f64(xT)[:, unstriped(offs)], 0, "e4m3")
    y = mxq(f64(w1), 0, "e4m3").T @ xq
    yc = y[:, unstriped(cen)]
    e = mxq(f64(w2), 0, "e4m3").T @ xq
    z = np.maximum(np.maximum(relu(yc + e[:, unstriped(pos1)]), relu(yc + e[:, unstriped(pos2)])), relu(yc + e[:, unstriped(pos3)]))
    return mxq(f64(w3), 0, "e4m3").T @ mxq(z, 0, "e4m3")

@@ -1,0 +1,165 @@
+from contextlib import ExitStack
+
+import concourse.mybir as mybir
+
+K, T, S, V, H, N = 512, 1024, 512, 256, 512, 128
+FLOPS = 2 * 2 * K * H * S + 2 * H * N * V
+
+F32 = mybir.dt.float32
+BF16 = mybir.dt.bfloat16
+U32 = mybir.dt.uint32
+U16 = mybir.dt.uint16
+U8 = mybir.dt.uint8
+FP8X4 = mybir.dt.float8_e4m3fn_x4
+ADD = mybir.AluOpType.add
+MAX = mybir.AluOpType.max
+COPY = mybir.ActivationFunctionType.Copy
+RELU = mybir.ActivationFunctionType.Relu
+
+P = 128
+PACK = 4
+HALF_S = S // 2
+HALF_H = H // 2
+HALF_V = V // 2
+
+
+def tile_picked_edgecv_relu_e_kernel(tc, xT, w1, w2, w3, offs, cen, pos1, pos2, pos3, out):
+    nc = tc.nc
+    with ExitStack() as ctx:
+        sb = ctx.enter_context(tc.tile_pool(name="sb", bufs=1))
+        ps = ctx.enter_context(tc.psum_pool(name="ps", bufs=1))
+
+        def load_list(name, src):
+            t = sb.tile(list(src.shape), U16, name=name)
+            nc.sync.dma_start(t[:], src)
+            return t
+
+        def load(name, shape, src):
+            t = sb.tile(shape, F32, name=name)
+            nc.sync.dma_start(t[:], src)
+            return t
+
+        def quantize(codes, scales, src):
+            nc.vector.quantize_mx(out=codes.bitcast(FP8X4), scales=scales, in_=src)
+
+        def mm(acc, wq, wsc, xq, xsc):
+            nc.tensor.matmul_mx(out=acc, lhsT=wq.bitcast(FP8X4), lhsT_scale=wsc,
+                                rhs=xq.bitcast(FP8X4), rhs_scale=xsc, start=True, stop=True)
+
+        x_rows = xT.rearrange("(p j) c -> p j c", j=PACK)
+        w1_rows = w1.rearrange("(p j) c -> p j c", j=PACK)
+        w2_rows = w2.rearrange("(p j) c -> p j c", j=PACK)
+        w3_rows = w3.rearrange("(p j) c -> p j c", j=PACK)
+
+        x_plane = [load("x0", [P, T], x_rows[:, 0, :])]
+        offs_t = load_list("offs_t", offs)
+        for j in range(1, PACK):
+            x_plane.append(load("x%d" % j, [P, T], x_rows[:, j, :]))
+        w2_raw = [load("w2r%d" % a, [P, PACK, HALF_H], w2_rows[:, :, a * HALF_H:(a + 1) * HALF_H]) for a in range(2)]
+        pos_t = [load_list("pos%d_t" % d, src) for d, src in enumerate((pos1, pos2, pos3))]
+        w1_raw = load("w1r", [P, PACK, H], w1_rows)
+        cen_t = load_list("cen_t", cen)
+        w3_raw = load("w3r", [P, PACK, N], w3_rows)
+
+        x_pair = [sb.tile([P, 2, S], F32, name="xpair%d" % u) for u in range(2)]
+        xb = sb.tile([P, S, PACK], BF16, name="xb", align_bytes=64)
+        xq = sb.tile([P, S], U32, name="xq", align_bytes=64)
+        xs = sb.tile([P, S], U8, name="xs", align_bytes=64)
+        for j in range(3):
+            nc.vector.tensor_copy(x_pair[j // 2][:, j % 2, :], x_plane[j][:].indirect(offs_t[:]))
+        nc.scalar.activation(xb[:, :, 0:2], x_pair[0][:].rearrange("p j c -> p c j"), COPY)
+        for a in range(2):
+            nc.vector.tensor_copy(x_pair[1][:, 1, a * HALF_S:(a + 1) * HALF_S],
+                                  x_plane[3][:].indirect(offs_t[:, a * 16:(a + 1) * 16]))
+        for a in range(2):
+            cols = slice(a * HALF_S, (a + 1) * HALF_S)
+            nc.vector.tensor_copy(xb[:, cols, 2:4], x_pair[1][:, :, cols].rearrange("p j c -> p c j"))
+
+        w2b = sb.tile([P, PACK, P, PACK], BF16, name="w2b", align_bytes=64)
+        w2q = sb.tile([P, H], U32, name="w2q", align_bytes=64)
+        w2s = sb.tile([P, H], U8, name="w2s", align_bytes=64)
+        hm = HALF_H // PACK
+        nc.scalar.copy(w2b[:, :, 0:hm, :].rearrange("p t m j -> p m j t"),
+                       w2_raw[0][:].rearrange("p j (m t) -> p m j t", t=PACK))
+        w2_late = w2_raw[1][:].rearrange("p j (m t) -> p m j t", t=PACK)
+        nc.scalar.copy(w2b[:, 0, hm:, :], w2_late[:, :, :, 0])
+        nc.scalar.copy(w2b[:, 1:, hm:, :].rearrange("p t m j -> p m j t"), w2_late[:, :, :, 1:])
+
+        def quant_w(wb, wq, wsc, t):
+            quantize(wq[:, t * P:(t + 1) * P], wsc[:, t * P:(t + 1) * P], wb[:, t, :, :].rearrange("p m j -> p (m j)"))
+
+        for a in range(2):
+            cols = slice(a * HALF_S, (a + 1) * HALF_S)
+            quantize(xq[:, cols], xs[:, cols], xb[:, cols, :].rearrange("p c j -> p (c j)"))
+        quant_w(w2b, w2q, w2s, 0)
+
+        e = [sb.tile([P, S], F32, name="e%d" % t) for t in range(PACK)]
+        y = [sb.tile([P, S], F32, name="y%d" % t) for t in range(PACK)]
+        for a in range(2):
+            cols = slice(a * HALF_S, (a + 1) * HALF_S)
+            acc = ps.tile([P, HALF_S], F32, name="first%d" % a)
+            mm(acc[:], w2q[:, 0:P], w2s[:, 0:P], xq[:, cols], xs[:, cols])
+            nc.scalar.copy(e[0][:, cols], acc[:])
+        for t in range(1, PACK):
+            quant_w(w2b, w2q, w2s, t)
+
+        def product(dst, wq, wsc, t):
+            acc = ps.tile([P, S], F32, name="acc", bufs=4)
+            mm(acc[:], wq[:, t * P:(t + 1) * P], wsc[:, t * P:(t + 1) * P], xq[:], xs[:])
+            nc.scalar.copy(dst[:], acc[:])
+
+        for t in range(1, PACK):
+            product(e[t], w2q, w2s, t)
+
+        w1b = sb.tile([P, PACK, P, PACK], BF16, name="w1b", align_bytes=64)
+        w1q = sb.tile([P, H], U32, name="w1q", align_bytes=64)
+        w1s = sb.tile([P, H], U8, name="w1s", align_bytes=64)
+        w1_view = w1_raw[:].rearrange("p j (m t) -> p m j t", t=PACK)
+        for a in range(2):
+            nc.scalar.copy(w1b[:, :, a * hm:(a + 1) * hm, :].rearrange("p t m j -> p m j t"),
+                           w1_view[:, a * hm:(a + 1) * hm, :, :])
+        w3b = sb.tile([P, N, PACK], BF16, name="w3b", align_bytes=64)
+        w3q = sb.tile([P, N], U32, name="w3q", align_bytes=64)
+        w3s = sb.tile([P, N], U8, name="w3s", align_bytes=64)
+        nc.scalar.copy(w3b[:], w3_raw[:].rearrange("p j n -> p n j"))
+
+        g = [sb.tile([P, 3, V], F32, name="g%d" % t) for t in range(PACK)]
+        m12 = [sb.tile([P, V], F32, name="m12_%d" % t) for t in range(PACK)]
+        best = [sb.tile([P, V], F32, name="best%d" % t) for t in range(PACK)]
+
+        def fetch(t, d):
+            nc.vector.tensor_copy(g[t][:, d, :], e[t][:].indirect(pos_t[d][:]))
+
+        for t in range(PACK):
+            fetch(t, 0)
+            if t > 0:
+                nc.vector.tensor_tensor(best[t - 1][:], m12[t - 1][:], g[t - 1][:, 2, :], MAX)
+            fetch(t, 1)
+            fetch(t, 2)
+            nc.vector.tensor_tensor(m12[t][:], g[t][:, 0, :], g[t][:, 1, :], MAX)
+            if t == 1:
+                quantize(w1q[:], w1s[:], w1b[:].rearrange("p t m j -> p (t m j)"))
+                for tt in range(PACK):
+                    product(y[tt], w1q, w1s, tt)
+        quantize(w3q[:], w3s[:], w3b[:].rearrange("p n j -> p (n j)"))
+        nc.vector.tensor_tensor(best[3][:], m12[3][:], g[3][:, 2, :], MAX)
+
+        zq, zs, zb = [], [], []
+        for a in range(2):
+            cols = slice(a * HALF_V, (a + 1) * HALF_V)
+            s = sb.tile([P, PACK, HALF_V], F32, name="s%d" % a)
+            for t in range(PACK):
+                nc.vector.tensor_tensor(s[:, t, :], y[t][:].indirect(cen_t[:, a * 8:(a + 1) * 8]), best[t][:, cols], ADD)
+            z = sb.tile([P, HALF_V, PACK], BF16, name="zb%d" % a, align_bytes=64)
+            nc.scalar.activation(z[:], s[:].rearrange("p t v -> p v t"), RELU)
+            zb.append(z)
+        for a in range(2):
+            cols = slice(a * HALF_V, (a + 1) * HALF_V)
+            q = sb.tile([P, HALF_V], U32, name="zq%d" % a, align_bytes=64)
+            sc = sb.tile([P, HALF_V], U8, name="zs%d" % a, align_bytes=64)
+            quantize(q[:], sc[:], zb[a][:].rearrange("p v t -> p (v t)"))
+            acc = ps.tile([P, HALF_V], F32, name="last%d" % a)
+            mm(acc[:], w3q[:], w3s[:], q[:], sc[:])
+            o = sb.tile([P, HALF_V], F32, name="o%d" % a)
+            nc.scalar.copy(o[:], acc[:])
+            nc.sync.dma_start(out[:, cols], o[:])

@@ -49,17 +49,19 @@ def tile_picked_edgecv_relu_e_kernel(tc, xT, w1, w2, w3, offs, cen, pos1, pos2, 
         x_rows = xT.rearrange("(p j) c -> p j c", j=PACK)
         w1_rows = w1.rearrange("(p j) c -> p j c", j=PACK)
         w2_rows = w2.rearrange("(p j) c -> p j c", j=PACK)
-        w3_rows = w3.rearrange("(p j) c -> p j c", j=PACK)
+        w3_rows = w3.rearrange("(g t b) n -> b g t n", t=PACK, b=2)
 
         x_plane = [load("x0", [P, T], x_rows[:, 0, :])]
         offs_t = load_list("offs_t", offs)
         for j in range(1, PACK):
             x_plane.append(load("x%d" % j, [P, T], x_rows[:, j, :]))
-        w2_raw = [load("w2r%d" % a, [P, PACK, HALF_H], w2_rows[:, :, a * HALF_H:(a + 1) * HALF_H]) for a in range(2)]
+        w2_raw = load("w2r", [P, PACK, H], w2_rows)
         pos_t = [load_list("pos%d_t" % d, src) for d, src in enumerate((pos1, pos2, pos3))]
         w1_raw = load("w1r", [P, PACK, H], w1_rows)
         cen_t = load_list("cen_t", cen)
-        w3_raw = load("w3r", [P, PACK, N], w3_rows)
+        w3_raw = sb.tile([P, PACK, N], F32, name="w3r")
+        for b in range(2):
+            nc.sync.dma_start(w3_raw[b:P:2, :, :], w3_rows[b])
 
         x_pair = [sb.tile([P, 2, S], F32, name="xpair%d" % u) for u in range(2)]
         xb = sb.tile([P, S, PACK], BF16, name="xb", align_bytes=64)
@@ -75,91 +77,109 @@ def tile_picked_edgecv_relu_e_kernel(tc, xT, w1, w2, w3, offs, cen, pos1, pos2, 
             cols = slice(a * HALF_S, (a + 1) * HALF_S)
             nc.vector.tensor_copy(xb[:, cols, 2:4], x_pair[1][:, :, cols].rearrange("p j c -> p c j"))
 
-        w2b = sb.tile([P, PACK, P, PACK], BF16, name="w2b", align_bytes=64)
-        w2q = sb.tile([P, H], U32, name="w2q", align_bytes=64)
-        w2s = sb.tile([P, H], U8, name="w2s", align_bytes=64)
-        hm = HALF_H // PACK
-        nc.scalar.copy(w2b[:, :, 0:hm, :].rearrange("p t m j -> p m j t"),
-                       w2_raw[0][:].rearrange("p j (m t) -> p m j t", t=PACK))
-        w2_late = w2_raw[1][:].rearrange("p j (m t) -> p m j t", t=PACK)
-        nc.scalar.copy(w2b[:, 0, hm:, :], w2_late[:, :, :, 0])
-        nc.scalar.copy(w2b[:, 1:, hm:, :].rearrange("p t m j -> p m j t"), w2_late[:, :, :, 1:])
+        def weight_tiles(name):
+            wb = sb.tile([P, PACK, P * PACK], BF16, name=name + "b", align_bytes=64)
+            wq = sb.tile([P, H], U32, name=name + "q", align_bytes=64)
+            wsc = sb.tile([P, H], U8, name=name + "s", align_bytes=64)
+            return wb, wq, wsc
 
-        def quant_w(wb, wq, wsc, t):
-            quantize(wq[:, t * P:(t + 1) * P], wsc[:, t * P:(t + 1) * P], wb[:, t, :, :].rearrange("p m j -> p (m j)"))
+        def cast_w(wb, raw, t):
+            nc.scalar.copy(wb[:, t, :].rearrange("p (g b j) -> p g j b", b=2, j=PACK),
+                           raw[:].rearrange("p j (g t b) -> p t g j b", t=PACK, b=2)[:, t])
 
+        def quant_w(wb, wq, wsc, t0, t1):
+            quantize(wq[:, t0 * P:t1 * P], wsc[:, t0 * P:t1 * P], wb[:, t0:t1, :].rearrange("p t c -> p (t c)"))
+
+        w2b, w2q, w2s = weight_tiles("w2")
+        cast_w(w2b, w2_raw, 0)
+        cast_w(w2b, w2_raw, 1)
         for a in range(2):
             cols = slice(a * HALF_S, (a + 1) * HALF_S)
             quantize(xq[:, cols], xs[:, cols], xb[:, cols, :].rearrange("p c j -> p (c j)"))
-        quant_w(w2b, w2q, w2s, 0)
+        quant_w(w2b, w2q, w2s, 0, 1)
 
         e = [sb.tile([P, S], F32, name="e%d" % t) for t in range(PACK)]
         y = [sb.tile([P, S], F32, name="y%d" % t) for t in range(PACK)]
         for a in range(2):
             cols = slice(a * HALF_S, (a + 1) * HALF_S)
-            acc = ps.tile([P, HALF_S], F32, name="first%d" % a)
+            acc = ps.tile([P, HALF_S], F32, name="half", bufs=2)
             mm(acc[:], w2q[:, 0:P], w2s[:, 0:P], xq[:, cols], xs[:, cols])
             nc.scalar.copy(e[0][:, cols], acc[:])
-        for t in range(1, PACK):
-            quant_w(w2b, w2q, w2s, t)
 
         def product(dst, wq, wsc, t):
-            acc = ps.tile([P, S], F32, name="acc", bufs=4)
+            acc = ps.tile([P, S], F32, name="acc", bufs=3)
             mm(acc[:], wq[:, t * P:(t + 1) * P], wsc[:, t * P:(t + 1) * P], xq[:], xs[:])
             nc.scalar.copy(dst[:], acc[:])
 
-        for t in range(1, PACK):
+        quant_w(w2b, w2q, w2s, 1, 2)
+        product(e[1], w2q, w2s, 1)
+        cast_w(w2b, w2_raw, 2)
+        cast_w(w2b, w2_raw, 3)
+        quant_w(w2b, w2q, w2s, 2, 4)
+        for t in (2, 3):
             product(e[t], w2q, w2s, t)
 
-        w1b = sb.tile([P, PACK, P, PACK], BF16, name="w1b", align_bytes=64)
-        w1q = sb.tile([P, H], U32, name="w1q", align_bytes=64)
-        w1s = sb.tile([P, H], U8, name="w1s", align_bytes=64)
-        w1_view = w1_raw[:].rearrange("p j (m t) -> p m j t", t=PACK)
-        for a in range(2):
-            nc.scalar.copy(w1b[:, :, a * hm:(a + 1) * hm, :].rearrange("p t m j -> p m j t"),
-                           w1_view[:, a * hm:(a + 1) * hm, :, :])
+        w1b, w1q, w1s = weight_tiles("w1")
+        for t in range(PACK):
+            cast_w(w1b, w1_raw, t)
         w3b = sb.tile([P, N, PACK], BF16, name="w3b", align_bytes=64)
         w3q = sb.tile([P, N], U32, name="w3q", align_bytes=64)
         w3s = sb.tile([P, N], U8, name="w3s", align_bytes=64)
         nc.scalar.copy(w3b[:], w3_raw[:].rearrange("p j n -> p n j"))
 
-        g = [sb.tile([P, 3, V], F32, name="g%d" % t) for t in range(PACK)]
-        m12 = [sb.tile([P, V], F32, name="m12_%d" % t) for t in range(PACK)]
-        best = [sb.tile([P, V], F32, name="best%d" % t) for t in range(PACK)]
+        left = [sb.tile([P, 3 * V], F32, name="left%d" % t) for t in range(PACK + 1)]
+        first = sb.tile([P, 2 * V], F32, name="first")
 
-        def fetch(t, d):
-            nc.vector.tensor_copy(g[t][:, d, :], e[t][:].indirect(pos_t[d][:]))
+        def fetch(dst, t, d):
+            nc.vector.tensor_copy(dst, e[t][:].indirect(pos_t[d][:]))
 
-        for t in range(PACK):
-            fetch(t, 0)
-            if t > 0:
-                nc.vector.tensor_tensor(best[t - 1][:], m12[t - 1][:], g[t - 1][:, 2, :], MAX)
-            fetch(t, 1)
-            fetch(t, 2)
-            nc.vector.tensor_tensor(m12[t][:], g[t][:, 0, :], g[t][:, 1, :], MAX)
-            if t == 1:
-                quantize(w1q[:], w1s[:], w1b[:].rearrange("p t m j -> p (t m j)"))
+        fetch(first[:, 0:V], 0, 0)
+        fetch(first[:, V:], 0, 1)
+        right = sb.tile([P, 2 * V], F32, name="right0")
+        fetch(right[:, 0:V], 0, 2)
+        nc.vector.tensor_tensor(left[0][:, V:2 * V], first[:, 0:V], first[:, V:], MAX)
+        for t in range(1, PACK):
+            fetch(left[t - 1][:, 2 * V:], t, 0)
+            fetch(right[:, V:], t, 1)
+            if t == 2:
+                quant_w(w1b, w1q, w1s, 0, 4)
                 for tt in range(PACK):
                     product(y[tt], w1q, w1s, tt)
+                nxt = sb.tile([P, 2 * V], F32, name="w1b", align_bytes=64)
+            else:
+                nxt = sb.tile([P, 2 * V], F32, name="right%d" % t)
+            fetch(nxt[:, 0:V], t, 2)
+            nc.vector.tensor_tensor(left[t][:, 0:2 * V], left[t - 1][:, V:], right[:], MAX)
+            right = nxt
         quantize(w3q[:], w3s[:], w3b[:].rearrange("p n j -> p (n j)"))
-        nc.vector.tensor_tensor(best[3][:], m12[3][:], g[3][:, 2, :], MAX)
+        nc.vector.tensor_tensor(left[PACK][:, 0:V], left[PACK - 1][:, V:2 * V], right[:, 0:V], MAX)
 
-        zq, zs, zb = [], [], []
-        for a in range(2):
-            cols = slice(a * HALF_V, (a + 1) * HALF_V)
-            s = sb.tile([P, PACK, HALF_V], F32, name="s%d" % a)
-            for t in range(PACK):
-                nc.vector.tensor_tensor(s[:, t, :], y[t][:].indirect(cen_t[:, a * 8:(a + 1) * 8]), best[t][:, cols], ADD)
-            z = sb.tile([P, HALF_V, PACK], BF16, name="zb%d" % a, align_bytes=64)
-            nc.scalar.activation(z[:], s[:].rearrange("p t v -> p v t"), RELU)
-            zb.append(z)
-        for a in range(2):
-            cols = slice(a * HALF_V, (a + 1) * HALF_V)
-            q = sb.tile([P, HALF_V], U32, name="zq%d" % a, align_bytes=64)
-            sc = sb.tile([P, HALF_V], U8, name="zs%d" % a, align_bytes=64)
-            quantize(q[:], sc[:], zb[a][:].rearrange("p v t -> p (v t)"))
-            acc = ps.tile([P, HALF_V], F32, name="last%d" % a)
+        pieces = [(0, 128), (128, 192), (192, 256)]
+        zb = []
+
+        def finish(i):
+            v0, v1 = pieces[i]
+            n = v1 - v0
+            q = sb.tile([P, n], U32, name="zq%d" % i, align_bytes=64)
+            sc = sb.tile([P, n], U8, name="zs%d" % i, align_bytes=64)
+            quantize(q[:], sc[:], zb[i][:].rearrange("p v t -> p (v t)"))
+            acc = ps.tile([P, n], F32, name="last%d" % i)
             mm(acc[:], w3q[:], w3s[:], q[:], sc[:])
-            o = sb.tile([P, HALF_V], F32, name="o%d" % a)
+            o = sb.tile([P, n], F32, name="o%d" % i)
             nc.scalar.copy(o[:], acc[:])
-            nc.sync.dma_start(out[:, cols], o[:])
+            nc.sync.dma_start(out[:, v0:v1], o[:])
+
+        for i, (v0, v1) in enumerate(pieces):
+            n = v1 - v0
+            s = sb.tile([P, PACK, n], F32, name="s%d" % i)
+            for t in range(PACK):
+                nc.vector.tensor_tensor(s[:, t, :], y[t][:].indirect(cen_t[:, v0 // 16:v1 // 16]), left[t + 1][:, v0:v1], ADD)
+            z = sb.tile([P, n, PACK], BF16, name="zb%d" % i, align_bytes=64)
+            zb.append(z)
+            if i > 0:
+                finish(i - 1)
+            if i < len(pieces) - 1:
+                nc.scalar.activation(z[:], s[:].rearrange("p t v -> p v t"), RELU)
+            else:
+                nc.vector.tensor_scalar_max(z[:], s[:].rearrange("p t v -> p v t"), 0.0)
+        finish(len(pieces) - 1)

@@ -1,6 +1,7 @@
 from contextlib import ExitStack
 
 import concourse.mybir as mybir
+from concourse.masks import make_identity
 
 K, T, S, V, H, N = 512, 1024, 512, 256, 512, 128
 FLOPS = 2 * 2 * K * H * S + 2 * H * N * V
@@ -63,123 +64,165 @@ def tile_picked_edgecv_relu_e_kernel(tc, xT, w1, w2, w3, offs, cen, pos1, pos2, 
         for b in range(2):
             nc.sync.dma_start(w3_raw[b:P:2, :, :], w3_rows[b])
 
-        x_pair = [sb.tile([P, 2, S], F32, name="xpair%d" % u) for u in range(2)]
-        xb = sb.tile([P, S, PACK], BF16, name="xb", align_bytes=64)
+        low = sb.tile([P, 2, S], F32, name="low")
+        high = sb.tile([P, 2, S], F32, name="high")
+        xb = [sb.tile([P, HALF_S, PACK], BF16, name="xb%d" % a, align_bytes=64) for a in range(2)]
         xq = sb.tile([P, S], U32, name="xq", align_bytes=64)
         xs = sb.tile([P, S], U8, name="xs", align_bytes=64)
-        for j in range(3):
-            nc.vector.tensor_copy(x_pair[j // 2][:, j % 2, :], x_plane[j][:].indirect(offs_t[:]))
-        nc.scalar.activation(xb[:, :, 0:2], x_pair[0][:].rearrange("p j c -> p c j"), COPY)
+        for j in range(2):
+            nc.vector.tensor_copy(low[:, j, :], x_plane[j][:].indirect(offs_t[:]))
         for a in range(2):
-            nc.vector.tensor_copy(x_pair[1][:, 1, a * HALF_S:(a + 1) * HALF_S],
-                                  x_plane[3][:].indirect(offs_t[:, a * 16:(a + 1) * 16]))
+            nc.scalar.activation(xb[a][:, :, 0:2], low[:, :, a * HALF_S:(a + 1) * HALF_S].rearrange("p j c -> p c j"), COPY)
+        nc.vector.tensor_copy(high[:, 0, :], x_plane[2][:].indirect(offs_t[:]))
         for a in range(2):
-            cols = slice(a * HALF_S, (a + 1) * HALF_S)
-            nc.vector.tensor_copy(xb[:, cols, 2:4], x_pair[1][:, :, cols].rearrange("p j c -> p c j"))
+            nc.vector.tensor_copy(high[:, 1, a * HALF_S:(a + 1) * HALF_S], x_plane[3][:].indirect(offs_t[:, a * 16:(a + 1) * 16]))
+        for a in range(2):
+            nc.vector.tensor_copy(xb[a][:, :, 2:4], high[:, :, a * HALF_S:(a + 1) * HALF_S].rearrange("p j c -> p c j"))
+        ident = sb.tile([P, P], F32, name="ident")
+        make_identity(nc, ident[:])
 
-        def weight_tiles(name):
-            wb = sb.tile([P, PACK, P * PACK], BF16, name=name + "b", align_bytes=64)
-            wq = sb.tile([P, H], U32, name=name + "q", align_bytes=64)
-            wsc = sb.tile([P, H], U8, name=name + "s", align_bytes=64)
-            return wb, wq, wsc
+        w1q = sb.tile([P, H], U32, name="w1q", align_bytes=64)
+        w1s = sb.tile([P, H], U8, name="w1s", align_bytes=64)
+        w2q = sb.tile([P, H], U32, name="w2q", align_bytes=64)
+        w2s = sb.tile([P, H], U8, name="w2s", align_bytes=64)
 
-        def cast_w(wb, raw, t):
-            nc.scalar.copy(wb[:, t, :].rearrange("p (g b j) -> p g j b", b=2, j=PACK),
+        def cast_w(dst, raw, t):
+            nc.scalar.copy(dst.rearrange("p (g b j) -> p g j b", b=2, j=PACK),
                            raw[:].rearrange("p j (g t b) -> p t g j b", t=PACK, b=2)[:, t])
 
-        def quant_w(wb, wq, wsc, t0, t1):
-            quantize(wq[:, t0 * P:t1 * P], wsc[:, t0 * P:t1 * P], wb[:, t0:t1, :].rearrange("p t c -> p (t c)"))
+        w2b = [sb.tile([P, H], BF16, name="w2b%d" % t, align_bytes=64) for t in range(PACK)]
+        w1b = [sb.tile([P, 2 * H], BF16, name="w1b%d" % u, align_bytes=64) for u in range(2)]
 
-        w2b, w2q, w2s = weight_tiles("w2")
-        cast_w(w2b, w2_raw, 0)
-        cast_w(w2b, w2_raw, 1)
+        def prepare_w2(t):
+            cast_w(w2b[t][:], w2_raw, t)
+            quantize(w2q[:, t * P:(t + 1) * P], w2s[:, t * P:(t + 1) * P], w2b[t][:])
+
+        def cast_w1(t):
+            cast_w(w1b[t // 2][:, (t % 2) * H:(t % 2 + 1) * H], w1_raw, t)
+
+        def cast_w1_pair(u):
+            nc.scalar.copy(w1b[u][:].rearrange("p (t g b j) -> p t g j b", t=2, b=2, j=PACK),
+                           w1_raw[:].rearrange("p j (g t b) -> p t g j b", t=PACK, b=2)[:, 2 * u:2 * u + 2])
+
+        def quant_w1(u):
+            quantize(w1q[:, u * 2 * P:(u + 1) * 2 * P], w1s[:, u * 2 * P:(u + 1) * 2 * P], w1b[u][:])
+
         for a in range(2):
             cols = slice(a * HALF_S, (a + 1) * HALF_S)
-            quantize(xq[:, cols], xs[:, cols], xb[:, cols, :].rearrange("p c j -> p (c j)"))
-        quant_w(w2b, w2q, w2s, 0, 1)
+            quantize(xq[:, cols], xs[:, cols], xb[a][:].rearrange("p c j -> p (c j)"))
+        for t in range(3):
+            prepare_w2(t)
 
         e = [sb.tile([P, S], F32, name="e%d" % t) for t in range(PACK)]
         y = [sb.tile([P, S], F32, name="y%d" % t) for t in range(PACK)]
         for a in range(2):
             cols = slice(a * HALF_S, (a + 1) * HALF_S)
-            acc = ps.tile([P, HALF_S], F32, name="half", bufs=2)
+            acc = ps.tile([P, HALF_S], F32, name="bank%d" % a)
             mm(acc[:], w2q[:, 0:P], w2s[:, 0:P], xq[:, cols], xs[:, cols])
             nc.scalar.copy(e[0][:, cols], acc[:])
 
-        def product(dst, wq, wsc, t):
-            acc = ps.tile([P, S], F32, name="acc", bufs=3)
+        def product(dst, wq, wsc, t, bank):
+            acc = ps.tile([P, S], F32, name="bank%d" % bank)
             mm(acc[:], wq[:, t * P:(t + 1) * P], wsc[:, t * P:(t + 1) * P], xq[:], xs[:])
             nc.scalar.copy(dst[:], acc[:])
 
-        quant_w(w2b, w2q, w2s, 1, 2)
-        product(e[1], w2q, w2s, 1)
-        cast_w(w2b, w2_raw, 2)
-        cast_w(w2b, w2_raw, 3)
-        quant_w(w2b, w2q, w2s, 2, 4)
-        for t in (2, 3):
-            product(e[t], w2q, w2s, t)
+        def fetch(dst, src, lst):
+            nc.vector.tensor_copy(dst, src[:].indirect(lst[:]))
 
-        w1b, w1q, w1s = weight_tiles("w1")
-        for t in range(PACK):
-            cast_w(w1b, w1_raw, t)
-        w3b = sb.tile([P, N, PACK], BF16, name="w3b", align_bytes=64)
+        yc = [sb.tile([P, V], F32, name="yc%d" % t) for t in range(2)]
+        g = [[sb.tile([P, V], F32, name="g0_%d" % d)[:] for d in range(3)]]
+
+        product(e[1], w2q, w2s, 1, 2)
+        for d in range(3):
+            fetch(g[0][d], e[0], pos_t[d])
+        prepare_w2(3)
+        cast_w1_pair(0)
+        for t in range(2):
+            quantize(w1q[:, t * P:(t + 1) * P], w1s[:, t * P:(t + 1) * P], w1b[0][:, t * H:(t + 1) * H])
+        reused = w1b[0][:].bitcast(F32)
+        spare = sb.tile([P, V], F32, name="g1_2")
+        g.append([reused[:, :V], reused[:, V:], spare[:]])
+        for d in (2, 0, 1):
+            fetch(g[1][d], e[1], pos_t[d])
+        cast_w1_pair(1)
+        quant_w1(1)
+        for t in range(2):
+            product(y[t], w1q, w1s, t, t)
+            fetch(yc[t][:], y[t], cen_t)
+        product(e[2], w2q, w2s, 2, 0)
+        product(e[3], w2q, w2s, 3, 1)
+
+        first = sb.tile([P, 2 * V], F32, name="first", align_bytes=64)
+        left2 = sb.tile([P, 2 * V], F32, name="left2")
+        right2 = sb.tile([P, 2 * V], F32, name="right2")
+        left3 = sb.tile([P, 2 * V], F32, name="left3")
+        last3 = sb.tile([P, V], F32, name="last3")
+        best3 = sb.tile([P, V], F32, name="best3")
+        fetch(first[:, :V], e[2], pos_t[0])
+        fetch(first[:, V:], e[2], pos_t[1])
+        fetch(right2[:, :V], e[2], pos_t[2])
+        nc.vector.tensor_tensor(left2[:, :V], first[:, :V], first[:, V:], MAX)
+
+        edge = []
+        for d in range(3):
+            sT = ps.tile([P, 2, 2, P], F32, name="sT%d" % d)
+            for t in range(2):
+                for blk in range(2):
+                    cols = slice(blk * P, (blk + 1) * P)
+                    nc.tensor.matmul(sT[:, blk, t, :], yc[t][:, cols], ident[:], start=True, stop=False, is_transpose=True)
+                    nc.tensor.matmul(sT[:, blk, t, :], g[t][d][:, cols], ident[:], start=False, stop=True, is_transpose=True)
+            aT = sb.tile([P, 2 * P * 2], BF16, name="aT%d" % d)
+            nc.scalar.activation(aT[:].rearrange("v (b p e) -> v b p e", b=2, e=2), sT[:].rearrange("v b e p -> v b p e"), RELU)
+            edge.append(aT)
+        for t in (2, 3):
+            product(y[t], w1q, w1s, t, t - 2)
+
+        w3b = sb.tile([P, N, PACK], BF16, name="first", align_bytes=64)
         w3q = sb.tile([P, N], U32, name="w3q", align_bytes=64)
         w3s = sb.tile([P, N], U8, name="w3s", align_bytes=64)
         nc.scalar.copy(w3b[:], w3_raw[:].rearrange("p j n -> p n j"))
 
-        left = [sb.tile([P, 3 * V], F32, name="left%d" % t) for t in range(PACK + 1)]
-        first = sb.tile([P, 2 * V], F32, name="first")
-
-        def fetch(dst, t, d):
-            nc.vector.tensor_copy(dst, e[t][:].indirect(pos_t[d][:]))
-
-        fetch(first[:, 0:V], 0, 0)
-        fetch(first[:, V:], 0, 1)
-        right = sb.tile([P, 2 * V], F32, name="right0")
-        fetch(right[:, 0:V], 0, 2)
-        nc.vector.tensor_tensor(left[0][:, V:2 * V], first[:, 0:V], first[:, V:], MAX)
-        for t in range(1, PACK):
-            fetch(left[t - 1][:, 2 * V:], t, 0)
-            fetch(right[:, V:], t, 1)
-            if t == 2:
-                quant_w(w1b, w1q, w1s, 0, 4)
-                for tt in range(PACK):
-                    product(y[tt], w1q, w1s, tt)
-                nxt = sb.tile([P, 2 * V], F32, name="w1b", align_bytes=64)
-            else:
-                nxt = sb.tile([P, 2 * V], F32, name="right%d" % t)
-            fetch(nxt[:, 0:V], t, 2)
-            nc.vector.tensor_tensor(left[t][:, 0:2 * V], left[t - 1][:, V:], right[:], MAX)
-            right = nxt
+        fetch(left2[:, V:], e[3], pos_t[0])
+        fetch(right2[:, V:], e[3], pos_t[1])
+        fetch(last3[:], e[3], pos_t[2])
+        two = sb.tile([P, 2 * V], BF16, name="two")
+        nc.vector.tensor_tensor(two[:], edge[0][:], edge[1][:], MAX)
+        nc.vector.tensor_tensor(left3[:], left2[:], right2[:], MAX)
+        zT = sb.tile([P, 2 * V], BF16, name="zT")
+        nc.vector.tensor_tensor(zT[:], two[:], edge[2][:], MAX)
+        nc.vector.tensor_tensor(best3[:], left3[:, V:], last3[:], MAX)
         quantize(w3q[:], w3s[:], w3b[:].rearrange("p n j -> p (n j)"))
-        nc.vector.tensor_tensor(left[PACK][:, 0:V], left[PACK - 1][:, V:2 * V], right[:, 0:V], MAX)
+        back = ps.tile([P, V], F32, name="back")
+        zT_words = zT[:].bitcast(F32)
+        for blk in range(2):
+            cols = slice(blk * P, (blk + 1) * P)
+            nc.tensor.transpose(back[:, cols], zT_words[:, cols], ident[:])
 
-        pieces = [(0, 128), (128, 192), (192, 256)]
-        zb = []
+        pieces = [(0, 128), (128, 256)]
+        zb = [sb.tile([P, (v1 - v0) * PACK], BF16, name="zb%d" % i, align_bytes=64) for i, (v0, v1) in enumerate(pieces)]
+        best = [left3[:, :V], best3[:]]
 
         def finish(i):
             v0, v1 = pieces[i]
             n = v1 - v0
             q = sb.tile([P, n], U32, name="zq%d" % i, align_bytes=64)
             sc = sb.tile([P, n], U8, name="zs%d" % i, align_bytes=64)
-            quantize(q[:], sc[:], zb[i][:].rearrange("p v t -> p (v t)"))
-            acc = ps.tile([P, n], F32, name="last%d" % i)
+            quantize(q[:], sc[:], zb[i][:])
+            acc = ps.tile([P, n], F32, name="bank%d" % i)
             mm(acc[:], w3q[:], w3s[:], q[:], sc[:])
             o = sb.tile([P, n], F32, name="o%d" % i)
             nc.scalar.copy(o[:], acc[:])
             nc.sync.dma_start(out[:, v0:v1], o[:])
 
+        s = [sb.tile([P, 2, v1 - v0], F32, name=("s0", "w3r")[i]) for i, (v0, v1) in enumerate(pieces)]
         for i, (v0, v1) in enumerate(pieces):
-            n = v1 - v0
-            s = sb.tile([P, PACK, n], F32, name="s%d" % i)
-            for t in range(PACK):
-                nc.vector.tensor_tensor(s[:, t, :], y[t][:].indirect(cen_t[:, v0 // 16:v1 // 16]), left[t + 1][:, v0:v1], ADD)
-            z = sb.tile([P, n, PACK], BF16, name="zb%d" % i, align_bytes=64)
-            zb.append(z)
-            if i > 0:
-                finish(i - 1)
+            for t in range(2):
+                nc.vector.tensor_tensor(s[i][:, t, :], y[2 + t][:].indirect(cen_t[:, v0 // 16:v1 // 16]), best[t][:, v0:v1], ADD)
+            nc.scalar.copy(zb[i][:].bitcast(F32).rearrange("p (v u) -> p v u", u=2)[:, :, 0], back[:, v0:v1])
+            pair = zb[i][:].rearrange("p (v t) -> p v t", t=PACK)[:, :, 2:4]
             if i < len(pieces) - 1:
-                nc.scalar.activation(z[:], s[:].rearrange("p t v -> p v t"), RELU)
+                nc.scalar.activation(pair, s[i][:].rearrange("p t v -> p v t"), RELU)
             else:
-                nc.vector.tensor_scalar_max(z[:], s[:].rearrange("p t v -> p v t"), 0.0)
-        finish(len(pieces) - 1)
+                finish(0)
+                nc.vector.tensor_scalar_max(pair, s[i][:].rearrange("p t v -> p v t"), 0.0)
+        finish(1)

@@ -18,10 +18,15 @@ COPY = mybir.ActivationFunctionType.Copy
 RELU = mybir.ActivationFunctionType.Relu
 
 P = 128
-PACK = 4
-HALF_S = S // 2
-HALF_H = H // 2
-HALF_V = V // 2
+SLOTS = 4
+NEIGHBOURS = 3
+PER_COLUMN = 16
+SECOND_PLANE = 4
+MX_ALIGN = 64
+
+
+def half(a, total):
+    return slice(a * total // 2, (a + 1) * total // 2)
 
 
 def tile_picked_edgecv_relu_e_kernel(tc, xT, w1, w2, w3, offs, cen, pos1, pos2, pos3, out):
@@ -30,199 +35,193 @@ def tile_picked_edgecv_relu_e_kernel(tc, xT, w1, w2, w3, offs, cen, pos1, pos2, 
         sb = ctx.enter_context(tc.tile_pool(name="sb", bufs=1))
         ps = ctx.enter_context(tc.psum_pool(name="ps", bufs=1))
 
-        def load_list(name, src):
-            t = sb.tile(list(src.shape), U16, name=name)
-            nc.sync.dma_start(t[:], src)
-            return t
+        def load(name, src, dtype):
+            tile = sb.tile(list(src.shape), dtype, name=name)
+            nc.sync.dma_start(tile[:], src)
+            return tile
 
-        def load(name, shape, src):
-            t = sb.tile(shape, F32, name=name)
-            nc.sync.dma_start(t[:], src)
-            return t
+        def quantize(codes, scales, values):
+            nc.vector.quantize_mx(out=codes.bitcast(FP8X4), scales=scales, in_=values)
 
-        def quantize(codes, scales, src):
-            nc.vector.quantize_mx(out=codes.bitcast(FP8X4), scales=scales, in_=src)
+        def product(dst, bank, w_codes, w_scales, m_codes, m_scales):
+            acc = ps.tile(list(dst.shape), F32, name="bank%d" % bank)
+            nc.tensor.matmul_mx(out=acc[:], lhsT=w_codes.bitcast(FP8X4), lhsT_scale=w_scales,
+                                rhs=m_codes.bitcast(FP8X4), rhs_scale=m_scales, start=True, stop=True)
+            nc.scalar.copy(dst, acc[:])
 
-        def mm(acc, wq, wsc, xq, xsc):
-            nc.tensor.matmul_mx(out=acc, lhsT=wq.bitcast(FP8X4), lhsT_scale=wsc,
-                                rhs=xq.bitcast(FP8X4), rhs_scale=xsc, start=True, stop=True)
+        def fetch(dst, window, offsets):
+            nc.vector.tensor_copy(dst, window[:].indirect(offsets))
 
-        x_rows = xT.rearrange("(p j) c -> p j c", j=PACK)
-        w1_rows = w1.rearrange("(p j) c -> p j c", j=PACK)
-        w2_rows = w2.rearrange("(p j) c -> p j c", j=PACK)
-        w3_rows = w3.rearrange("(g t b) n -> b g t n", t=PACK, b=2)
-
-        x_plane = [load("x0", [P, T], x_rows[:, 0, :])]
-        offs_t = load_list("offs_t", offs)
-        for j in range(1, PACK):
-            x_plane.append(load("x%d" % j, [P, T], x_rows[:, j, :]))
-        w2_raw = load("w2r", [P, PACK, H], w2_rows)
-        pos_t = [load_list("pos%d_t" % d, src) for d, src in enumerate((pos1, pos2, pos3))]
-        w1_raw = load("w1r", [P, PACK, H], w1_rows)
-        cen_t = load_list("cen_t", cen)
-        w3_raw = sb.tile([P, PACK, N], F32, name="w3r")
+        x_rows = xT.rearrange("(p j) c -> p j c", j=SLOTS)
+        w2_rows = w2.rearrange("(p j) c -> p j c", j=SLOTS)
+        x_plane = [load("x0", x_rows[:, 0, :], F32)]
+        offs_list = load("offs_list", offs, U16)
+        for j in range(1, SLOTS):
+            x_plane.append(load("x%d" % j, x_rows[:, j, :], F32))
+        w2_raw = [load("w2_raw%d" % a, w2_rows[:, :, half(a, H)], F32) for a in range(2)]
+        pos_list = [load("pos_list%d" % d, src, U16) for d, src in enumerate((pos1, pos2, pos3))]
+        w1_raw = load("w1_raw", w1.rearrange("(p j) c -> p j c", j=SLOTS), F32)
+        cen_list = load("cen_list", cen, U16)
+        w3_raw = sb.tile([P, SLOTS, N], F32, name="w3_raw")
+        w3_rows = w3.rearrange("(g t b) n -> b g t n", t=SLOTS, b=2)
         for b in range(2):
             nc.sync.dma_start(w3_raw[b:P:2, :, :], w3_rows[b])
 
-        low = sb.tile([P, 2, S], F32, name="low")
-        high = sb.tile([P, 2, S], F32, name="high")
-        xb = [sb.tile([P, HALF_S, PACK], BF16, name="xb%d" % a, align_bytes=64) for a in range(2)]
-        xq = sb.tile([P, S], U32, name="xq", align_bytes=64)
-        xs = sb.tile([P, S], U8, name="xs", align_bytes=64)
+        picked01 = sb.tile([P, 2, S], F32, name="picked01")
+        picked23 = sb.tile([P, 2, S], F32, name="picked23")
+        x_bf16 = [sb.tile([P, S // 2, SLOTS], BF16, name="x_bf16_%d" % a, align_bytes=MX_ALIGN) for a in range(2)]
+        x_codes = sb.tile([P, S], U32, name="x_codes", align_bytes=MX_ALIGN)
+        x_scales = sb.tile([P, S], U8, name="x_scales", align_bytes=MX_ALIGN)
         for j in range(2):
-            nc.vector.tensor_copy(low[:, j, :], x_plane[j][:].indirect(offs_t[:]))
+            fetch(picked01[:, j, :], x_plane[j], offs_list[:])
         for a in range(2):
-            nc.scalar.activation(xb[a][:, :, 0:2], low[:, :, a * HALF_S:(a + 1) * HALF_S].rearrange("p j c -> p c j"), COPY)
-        nc.vector.tensor_copy(high[:, 0, :], x_plane[2][:].indirect(offs_t[:]))
+            nc.scalar.activation(x_bf16[a][:, :, 0:2], picked01[:, :, half(a, S)].rearrange("p j c -> p c j"), COPY)
+        fetch(picked23[:, 0, :], x_plane[2], offs_list[:])
         for a in range(2):
-            nc.vector.tensor_copy(high[:, 1, a * HALF_S:(a + 1) * HALF_S], x_plane[3][:].indirect(offs_t[:, a * 16:(a + 1) * 16]))
+            fetch(picked23[:, 1, half(a, S)], x_plane[3], offs_list[:, half(a, S // PER_COLUMN)])
         for a in range(2):
-            nc.vector.tensor_copy(xb[a][:, :, 2:4], high[:, :, a * HALF_S:(a + 1) * HALF_S].rearrange("p j c -> p c j"))
-        ident = sb.tile([P, P], F32, name="ident")
-        make_identity(nc, ident[:])
+            nc.vector.tensor_copy(x_bf16[a][:, :, 2:4], picked23[:, :, half(a, S)].rearrange("p j c -> p c j"))
+        identity = sb.tile([P, P], F32, name="identity")
+        make_identity(nc, identity[:])
 
-        w1q = sb.tile([P, H], U32, name="w1q", align_bytes=64)
-        w1s = sb.tile([P, H], U8, name="w1s", align_bytes=64)
-        w2q = sb.tile([P, H], U32, name="w2q", align_bytes=64)
-        w2s = sb.tile([P, H], U8, name="w2s", align_bytes=64)
+        w1_codes = sb.tile([P, H], U32, name="w1_codes", align_bytes=MX_ALIGN)
+        w1_scales = sb.tile([P, H], U8, name="w1_scales", align_bytes=MX_ALIGN)
+        w2_codes = sb.tile([P, H], U32, name="w2_codes", align_bytes=MX_ALIGN)
+        w2_scales = sb.tile([P, H], U8, name="w2_scales", align_bytes=MX_ALIGN)
+        w2_scales23 = w1_scales[SECOND_PLANE:, half(0, H)]
 
-        def cast_w(dst, raw, t):
-            nc.scalar.copy(dst.rearrange("p (g b j) -> p g j b", b=2, j=PACK),
-                           raw[:].rearrange("p j (g t b) -> p t g j b", t=PACK, b=2)[:, t])
+        def round_tiles01(dst, raw):
+            nc.scalar.copy(dst.rearrange("p (g c j) -> p g j c", c=4, j=SLOTS),
+                           raw[:].rearrange("p j (g u c) -> p u g j c", u=2, c=4)[:, 0])
 
-        w2b = [sb.tile([P, H], BF16, name="w2b%d" % t, align_bytes=64) for t in range(PACK)]
-        w1b = [sb.tile([P, 2 * H], BF16, name="w1b%d" % u, align_bytes=64) for u in range(2)]
+        def round_tiles23(dst, raw):
+            nc.scalar.copy(dst, raw[:].rearrange("p j (g u s b) -> p u s g j b", u=2, s=2, b=2)[:, 1])
 
-        def prepare_w2(t):
-            cast_w(w2b[t][:], w2_raw, t)
-            quantize(w2q[:, t * P:(t + 1) * P], w2s[:, t * P:(t + 1) * P], w2b[t][:])
+        def tile_columns(t):
+            return slice(t * P, (t + 1) * P)
 
-        def cast_w1(t):
-            cast_w(w1b[t // 2][:, (t % 2) * H:(t % 2 + 1) * H], w1_raw, t)
-
-        def cast_w1_pair(u):
-            nc.scalar.copy(w1b[u][:].rearrange("p (t g b j) -> p t g j b", t=2, b=2, j=PACK),
-                           w1_raw[:].rearrange("p j (g t b) -> p t g j b", t=PACK, b=2)[:, 2 * u:2 * u + 2])
-
-        def quant_w1(u):
-            quantize(w1q[:, u * 2 * P:(u + 1) * 2 * P], w1s[:, u * 2 * P:(u + 1) * 2 * P], w1b[u][:])
+        w2_bf16 = [sb.tile([P, P * SLOTS], BF16, name="w2_bf16_%d" % t, align_bytes=MX_ALIGN) for t in range(2)]
+        w2_bf16_23 = sb.tile([P, 2 * P * SLOTS], BF16, name="w2_bf16_23", align_bytes=MX_ALIGN)
+        w1_bf16_01 = sb.tile([P, 2 * P * SLOTS], BF16, name="w1_bf16_01", align_bytes=MX_ALIGN)
+        w1_bf16_23 = sb.tile([P, 2 * P * SLOTS], BF16, name="w1_bf16_23", align_bytes=MX_ALIGN)
 
         for a in range(2):
-            cols = slice(a * HALF_S, (a + 1) * HALF_S)
-            quantize(xq[:, cols], xs[:, cols], xb[a][:].rearrange("p c j -> p (c j)"))
-        for t in range(3):
-            prepare_w2(t)
-
-        e = [sb.tile([P, S], F32, name="e%d" % t) for t in range(PACK)]
-        y = [sb.tile([P, S], F32, name="y%d" % t) for t in range(PACK)]
-        for a in range(2):
-            cols = slice(a * HALF_S, (a + 1) * HALF_S)
-            acc = ps.tile([P, HALF_S], F32, name="bank%d" % a)
-            mm(acc[:], w2q[:, 0:P], w2s[:, 0:P], xq[:, cols], xs[:, cols])
-            nc.scalar.copy(e[0][:, cols], acc[:])
-
-        def product(dst, wq, wsc, t, bank):
-            acc = ps.tile([P, S], F32, name="bank%d" % bank)
-            mm(acc[:], wq[:, t * P:(t + 1) * P], wsc[:, t * P:(t + 1) * P], xq[:], xs[:])
-            nc.scalar.copy(dst[:], acc[:])
-
-        def fetch(dst, src, lst):
-            nc.vector.tensor_copy(dst, src[:].indirect(lst[:]))
-
-        yc = [sb.tile([P, V], F32, name="yc%d" % t) for t in range(2)]
-        g = [[sb.tile([P, V], F32, name="g0_%d" % d)[:] for d in range(3)]]
-
-        product(e[1], w2q, w2s, 1, 2)
-        for d in range(3):
-            fetch(g[0][d], e[0], pos_t[d])
-        prepare_w2(3)
-        cast_w1_pair(0)
+            quantize(x_codes[:, half(a, S)], x_scales[:, half(a, S)], x_bf16[a][:].rearrange("p c j -> p (c j)"))
         for t in range(2):
-            quantize(w1q[:, t * P:(t + 1) * P], w1s[:, t * P:(t + 1) * P], w1b[0][:, t * H:(t + 1) * H])
-        reused = w1b[0][:].bitcast(F32)
-        spare = sb.tile([P, V], F32, name="g1_2")
-        g.append([reused[:, :V], reused[:, V:], spare[:]])
-        for d in (2, 0, 1):
-            fetch(g[1][d], e[1], pos_t[d])
-        cast_w1_pair(1)
-        quant_w1(1)
+            round_tiles01(w2_bf16[t][:], w2_raw[t])
+            quantize(w2_codes[:, tile_columns(t)], w2_scales[:, tile_columns(t)], w2_bf16[t][:])
+        w2_view23 = w2_bf16_23[:].rearrange("p (s a g b j) -> p a s g j b", s=2, a=2, b=2, j=SLOTS)
+        for a in range(2):
+            round_tiles23(w2_view23[:, a], w2_raw[a])
+        quantize(w2_codes[:, half(1, H)], w2_scales23, w2_bf16_23[:])
+
+        e = [sb.tile([P, S], F32, name=name, align_bytes=MX_ALIGN) for name in ("w2_bf16_1", "e1", "e2", "e3")]
+        y = [sb.tile([P, S], F32, name="y%d" % t) for t in range(SLOTS)]
+
+        def first_product(dst, bank, w_codes, w_scales):
+            product(dst[:], bank, w_codes, w_scales, x_codes[:], x_scales[:])
+
+        for a in range(2):
+            product(e[0][:, half(a, S)], a, w2_codes[:, tile_columns(0)], w2_scales[:, tile_columns(0)],
+                    x_codes[:, half(a, S)], x_scales[:, half(a, S)])
+
+        centre = [sb.tile([P, V], F32, name="centre%d" % t) for t in range(2)]
+        near0 = [sb.tile([P, V], F32, name="near0_%d" % d)[:] for d in range(NEIGHBOURS)]
+        first_product(e[1], 2, w2_codes[:, tile_columns(1)], w2_scales[:, tile_columns(1)])
+        for d in range(NEIGHBOURS):
+            fetch(near0[d], e[0], pos_list[d][:])
+        round_tiles01(w1_bf16_01[:], w1_raw)
         for t in range(2):
-            product(y[t], w1q, w1s, t, t)
-            fetch(yc[t][:], y[t], cen_t)
-        product(e[2], w2q, w2s, 2, 0)
-        product(e[3], w2q, w2s, 3, 1)
-
-        first = sb.tile([P, 2 * V], F32, name="first", align_bytes=64)
-        left2 = sb.tile([P, 2 * V], F32, name="left2")
-        right2 = sb.tile([P, 2 * V], F32, name="right2")
-        left3 = sb.tile([P, 2 * V], F32, name="left3")
-        last3 = sb.tile([P, V], F32, name="last3")
-        best3 = sb.tile([P, V], F32, name="best3")
-        fetch(first[:, :V], e[2], pos_t[0])
-        fetch(first[:, V:], e[2], pos_t[1])
-        fetch(right2[:, :V], e[2], pos_t[2])
-        nc.vector.tensor_tensor(left2[:, :V], first[:, :V], first[:, V:], MAX)
-
-        edge = []
-        for d in range(3):
-            sT = ps.tile([P, 2, 2, P], F32, name="sT%d" % d)
-            for t in range(2):
-                for blk in range(2):
-                    cols = slice(blk * P, (blk + 1) * P)
-                    nc.tensor.matmul(sT[:, blk, t, :], yc[t][:, cols], ident[:], start=True, stop=False, is_transpose=True)
-                    nc.tensor.matmul(sT[:, blk, t, :], g[t][d][:, cols], ident[:], start=False, stop=True, is_transpose=True)
-            aT = sb.tile([P, 2 * P * 2], BF16, name="aT%d" % d)
-            nc.scalar.activation(aT[:].rearrange("v (b p e) -> v b p e", b=2, e=2), sT[:].rearrange("v b e p -> v b p e"), RELU)
-            edge.append(aT)
+            quantize(w1_codes[:, tile_columns(t)], w1_scales[:, tile_columns(t)], w1_bf16_01[:, half(t, 2 * P * SLOTS)])
+        reused = w1_bf16_01[:].bitcast(F32)
+        near1_own = sb.tile([P, V], F32, name="near1_own")
+        near1 = [reused[:, :V], reused[:, V:], near1_own[:]]
+        fetch(near1[2], e[1], pos_list[2][:])
+        for d in range(2):
+            fetch(near1[d], e[1], pos_list[d][:])
+        round_tiles23(w1_bf16_23[:].rearrange("p (s g b j) -> p s g j b", s=2, b=2, j=SLOTS), w1_raw)
+        quantize(w1_codes[:, half(1, H)], w1_scales[:, half(1, H)], w1_bf16_23[:])
+        for t in range(2):
+            first_product(y[t], t, w1_codes[:, tile_columns(t)], w1_scales[:, tile_columns(t)])
+            fetch(centre[t][:], y[t], cen_list[:])
         for t in (2, 3):
-            product(y[t], w1q, w1s, t, t - 2)
+            first_product(e[t], 5 - t, w2_codes[:, tile_columns(t)], w2_scales23[:, tile_columns(t - 2)])
 
-        w3b = sb.tile([P, N, PACK], BF16, name="first", align_bytes=64)
-        w3q = sb.tile([P, N], U32, name="w3q", align_bytes=64)
-        w3s = sb.tile([P, N], U8, name="w3s", align_bytes=64)
-        nc.scalar.copy(w3b[:], w3_raw[:].rearrange("p j n -> p n j"))
+        near2_01 = sb.tile([P, 2 * V], F32, name="near2_01", align_bytes=MX_ALIGN)
+        join_left = sb.tile([P, 2 * V], F32, name="join_left")
+        join_right = sb.tile([P, 2 * V], F32, name="join_right")
+        joined = sb.tile([P, 2 * V], F32, name="joined")
+        near3_2 = sb.tile([P, V], F32, name="near3_2")
+        largest3 = sb.tile([P, V], F32, name="largest3")
+        fetch(near2_01[:, :V], e[2], pos_list[0][:])
+        fetch(near2_01[:, V:], e[2], pos_list[1][:])
+        fetch(join_right[:, :V], e[2], pos_list[2][:])
+        nc.vector.tensor_tensor(join_left[:, :V], near2_01[:, :V], near2_01[:, V:], MAX)
 
-        fetch(left2[:, V:], e[3], pos_t[0])
-        fetch(right2[:, V:], e[3], pos_t[1])
-        fetch(last3[:], e[3], pos_t[2])
-        two = sb.tile([P, 2 * V], BF16, name="two")
-        nc.vector.tensor_tensor(two[:], edge[0][:], edge[1][:], MAX)
-        nc.vector.tensor_tensor(left3[:], left2[:], right2[:], MAX)
-        zT = sb.tile([P, 2 * V], BF16, name="zT")
-        nc.vector.tensor_tensor(zT[:], two[:], edge[2][:], MAX)
-        nc.vector.tensor_tensor(best3[:], left3[:, V:], last3[:], MAX)
-        quantize(w3q[:], w3s[:], w3b[:].rearrange("p n j -> p (n j)"))
-        back = ps.tile([P, V], F32, name="back")
-        zT_words = zT[:].bitcast(F32)
-        for blk in range(2):
-            cols = slice(blk * P, (blk + 1) * P)
-            nc.tensor.transpose(back[:, cols], zT_words[:, cols], ident[:])
+        candidate = []
+        for d in range(NEIGHBOURS):
+            sums = ps.tile([P, 2, 2, P], F32, name="sums%d" % d)
+            for t, near in enumerate((near0, near1)):
+                for group in range(2):
+                    centres = half(group, V)
+                    nc.tensor.matmul(sums[:, group, t, :], centre[t][:, centres], identity[:],
+                                     start=True, stop=False, is_transpose=True)
+                    nc.tensor.matmul(sums[:, group, t, :], near[d][:, centres], identity[:],
+                                     start=False, stop=True, is_transpose=True)
+            rounded = sb.tile([P, 2 * P * 2], BF16, name="candidate%d" % d)
+            nc.scalar.activation(rounded[:].rearrange("v (x b s) -> v x b s", b=2, s=2),
+                                 sums[:].rearrange("v group t (r s b) -> v (group t r) b s", s=2, b=2), RELU)
+            candidate.append(rounded)
+        for t in (2, 3):
+            first_product(y[t], 5 - t, w1_codes[:, tile_columns(t)], w1_scales[:, tile_columns(t)])
 
-        pieces = [(0, 128), (128, 256)]
-        zb = [sb.tile([P, (v1 - v0) * PACK], BF16, name="zb%d" % i, align_bytes=64) for i, (v0, v1) in enumerate(pieces)]
-        best = [left3[:, :V], best3[:]]
+        w3_bf16 = sb.tile([P, N, SLOTS], BF16, name="near2_01", align_bytes=MX_ALIGN)
+        w3_codes = sb.tile([P, N], U32, name="w3_codes", align_bytes=MX_ALIGN)
+        w3_scales = sb.tile([P, N], U8, name="w3_scales", align_bytes=MX_ALIGN)
+        nc.scalar.copy(w3_bf16[:], w3_raw[:].rearrange("p t n -> p n t"))
 
-        def finish(i):
-            v0, v1 = pieces[i]
-            n = v1 - v0
-            q = sb.tile([P, n], U32, name="zq%d" % i, align_bytes=64)
-            sc = sb.tile([P, n], U8, name="zs%d" % i, align_bytes=64)
-            quantize(q[:], sc[:], zb[i][:])
-            acc = ps.tile([P, n], F32, name="bank%d" % i)
-            mm(acc[:], w3q[:], w3s[:], q[:], sc[:])
-            o = sb.tile([P, n], F32, name="o%d" % i)
-            nc.scalar.copy(o[:], acc[:])
-            nc.sync.dma_start(out[:, v0:v1], o[:])
+        fetch(join_left[:, V:], e[3], pos_list[0][:])
+        fetch(join_right[:, V:], e[3], pos_list[1][:])
+        fetch(near3_2[:], e[3], pos_list[2][:])
+        larger01 = sb.tile([P, 2 * V], BF16, name="larger01")
+        nc.vector.tensor_tensor(larger01[:], candidate[0][:], candidate[1][:], MAX)
+        nc.vector.tensor_tensor(joined[:], join_left[:], join_right[:], MAX)
+        z_turned = sb.tile([P, 2 * V], BF16, name="z_turned")
+        nc.vector.tensor_tensor(z_turned[:], larger01[:], candidate[2][:], MAX)
+        nc.vector.tensor_tensor(largest3[:], joined[:, V:], near3_2[:], MAX)
+        quantize(w3_codes[:], w3_scales[:], w3_bf16[:].rearrange("p n t -> p (n t)"))
 
-        s = [sb.tile([P, 2, v1 - v0], F32, name=("s0", "w3r")[i]) for i, (v0, v1) in enumerate(pieces)]
-        for i, (v0, v1) in enumerate(pieces):
-            for t in range(2):
-                nc.vector.tensor_tensor(s[i][:, t, :], y[2 + t][:].indirect(cen_t[:, v0 // 16:v1 // 16]), best[t][:, v0:v1], ADD)
-            nc.scalar.copy(zb[i][:].bitcast(F32).rearrange("p (v u) -> p v u", u=2)[:, :, 0], back[:, v0:v1])
-            pair = zb[i][:].rearrange("p (v t) -> p v t", t=PACK)[:, :, 2:4]
-            if i < len(pieces) - 1:
-                nc.scalar.activation(pair, s[i][:].rearrange("p t v -> p v t"), RELU)
-            else:
-                finish(0)
-                nc.vector.tensor_scalar_max(pair, s[i][:].rearrange("p t v -> p v t"), 0.0)
-        finish(1)
+        z_words = ps.tile([P, V], F32, name="z_words")
+        for group in range(2):
+            nc.tensor.transpose(z_words[:, half(group, V)], z_turned[:].bitcast(F32)[:, half(group, V)], identity[:])
+        z_bf16 = [sb.tile([P, V // 2 * SLOTS], BF16, name="z_bf16_%d" % group, align_bytes=MX_ALIGN) for group in range(2)]
+        for group in range(2):
+            nc.scalar.copy(z_bf16[group][:].bitcast(F32).rearrange("p (v u) -> p v u", u=2)[:, :, 0],
+                           z_words[:, half(group, V)])
+
+        largest = [joined[:, :V], largest3[:]]
+        summed = [sb.tile([P, 2, V // 2], F32, name="summed%d" % group) for group in range(2)]
+
+        def add_centres(group):
+            offsets = cen_list[:, half(group, V // PER_COLUMN)]
+            for s in range(2):
+                nc.vector.tensor_tensor(summed[group][:, s, :], y[2 + s][:].indirect(offsets),
+                                        largest[s][:, half(group, V)], ADD)
+
+        def slots23(group):
+            return z_bf16[group][:].rearrange("p (v t) -> p v t", t=SLOTS)[:, :, 2:4]
+
+        def last_product(group):
+            z_codes = sb.tile([P, V // 2], U32, name="z_codes%d" % group, align_bytes=MX_ALIGN)
+            z_scales = sb.tile([P, V // 2], U8, name="z_scales%d" % group, align_bytes=MX_ALIGN)
+            quantize(z_codes[:], z_scales[:], z_bf16[group][:])
+            result = sb.tile([P, V // 2], F32, name="result%d" % group)
+            product(result[:], group, w3_codes[:], w3_scales[:], z_codes[:], z_scales[:])
+            nc.sync.dma_start(out[:, half(group, V)], result[:])
+
+        add_centres(0)
+        nc.scalar.activation(slots23(0), summed[0][:].rearrange("p s v -> p v s"), RELU)
+        add_centres(1)
+        last_product(0)
+        nc.vector.tensor_scalar_max(slots23(1), summed[1][:].rearrange("p s v -> p v s"), 0.0)
+        last_product(1)

from contextlib import ExitStack

import concourse.mybir as mybir
from concourse.masks import make_identity

K, T, S, V, H, N = 512, 1024, 512, 256, 512, 128
FLOPS = 2 * 2 * K * H * S + 2 * H * N * V

F32 = mybir.dt.float32
BF16 = mybir.dt.bfloat16
U32 = mybir.dt.uint32
U16 = mybir.dt.uint16
U8 = mybir.dt.uint8
FP8X4 = mybir.dt.float8_e4m3fn_x4
ADD = mybir.AluOpType.add
MAX = mybir.AluOpType.max
COPY = mybir.ActivationFunctionType.Copy
RELU = mybir.ActivationFunctionType.Relu

P = 128
SLOTS = 4
NEIGHBOURS = 3
PER_COLUMN = 16
SECOND_PLANE = 4
MX_ALIGN = 64


def half(a, total):
    return slice(a * total // 2, (a + 1) * total // 2)


def tile_picked_edgecv_relu_e_kernel(tc, xT, w1, w2, w3, offs, cen, pos1, pos2, pos3, out):
    nc = tc.nc
    with ExitStack() as ctx:
        sb = ctx.enter_context(tc.tile_pool(name="sb", bufs=1))
        ps = ctx.enter_context(tc.psum_pool(name="ps", bufs=1))

        def load(name, src, dtype):
            tile = sb.tile(list(src.shape), dtype, name=name)
            nc.sync.dma_start(tile[:], src)
            return tile

        def quantize(codes, scales, values):
            nc.vector.quantize_mx(out=codes.bitcast(FP8X4), scales=scales, in_=values)

        def product(dst, bank, w_codes, w_scales, m_codes, m_scales):
            acc = ps.tile(list(dst.shape), F32, name="bank%d" % bank)
            nc.tensor.matmul_mx(out=acc[:], lhsT=w_codes.bitcast(FP8X4), lhsT_scale=w_scales,
                                rhs=m_codes.bitcast(FP8X4), rhs_scale=m_scales, start=True, stop=True)
            nc.scalar.copy(dst, acc[:])

        def fetch(dst, window, offsets):
            nc.vector.tensor_copy(dst, window[:].indirect(offsets))

        x_rows = xT.rearrange("(p j) c -> p j c", j=SLOTS)
        w2_rows = w2.rearrange("(p j) c -> p j c", j=SLOTS)
        x_plane = [load("x0", x_rows[:, 0, :], F32)]
        offs_list = load("offs_list", offs, U16)
        for j in range(1, SLOTS):
            x_plane.append(load("x%d" % j, x_rows[:, j, :], F32))
        w2_raw = [load("w2_raw%d" % a, w2_rows[:, :, half(a, H)], F32) for a in range(2)]
        pos_list = [load("pos_list%d" % d, src, U16) for d, src in enumerate((pos1, pos2, pos3))]
        w1_raw = load("w1_raw", w1.rearrange("(p j) c -> p j c", j=SLOTS), F32)
        cen_list = load("cen_list", cen, U16)
        w3_raw = sb.tile([P, SLOTS, N], F32, name="w3_raw")
        w3_rows = w3.rearrange("(g t b) n -> b g t n", t=SLOTS, b=2)
        for b in range(2):
            nc.sync.dma_start(w3_raw[b:P:2, :, :], w3_rows[b])

        picked01 = sb.tile([P, 2, S], F32, name="picked01")
        picked23 = sb.tile([P, 2, S], F32, name="picked23")
        x_bf16 = [sb.tile([P, S // 2, SLOTS], BF16, name="x_bf16_%d" % a, align_bytes=MX_ALIGN) for a in range(2)]
        x_codes = sb.tile([P, S], U32, name="x_codes", align_bytes=MX_ALIGN)
        x_scales = sb.tile([P, S], U8, name="x_scales", align_bytes=MX_ALIGN)
        for j in range(2):
            fetch(picked01[:, j, :], x_plane[j], offs_list[:])
        for a in range(2):
            nc.scalar.activation(x_bf16[a][:, :, 0:2], picked01[:, :, half(a, S)].rearrange("p j c -> p c j"), COPY)
        fetch(picked23[:, 0, :], x_plane[2], offs_list[:])
        for a in range(2):
            fetch(picked23[:, 1, half(a, S)], x_plane[3], offs_list[:, half(a, S // PER_COLUMN)])
        for a in range(2):
            nc.vector.tensor_copy(x_bf16[a][:, :, 2:4], picked23[:, :, half(a, S)].rearrange("p j c -> p c j"))
        identity = sb.tile([P, P], F32, name="identity")
        make_identity(nc, identity[:])

        w1_codes = sb.tile([P, H], U32, name="w1_codes", align_bytes=MX_ALIGN)
        w1_scales = sb.tile([P, H], U8, name="w1_scales", align_bytes=MX_ALIGN)
        w2_codes = sb.tile([P, H], U32, name="w2_codes", align_bytes=MX_ALIGN)
        w2_scales = sb.tile([P, H], U8, name="w2_scales", align_bytes=MX_ALIGN)
        w2_scales23 = w1_scales[SECOND_PLANE:, half(0, H)]

        def round_tiles01(dst, raw):
            nc.scalar.copy(dst.rearrange("p (g c j) -> p g j c", c=4, j=SLOTS),
                           raw[:].rearrange("p j (g u c) -> p u g j c", u=2, c=4)[:, 0])

        def round_tiles23(dst, raw):
            nc.scalar.copy(dst, raw[:].rearrange("p j (g u s b) -> p u s g j b", u=2, s=2, b=2)[:, 1])

        def tile_columns(t):
            return slice(t * P, (t + 1) * P)

        w2_bf16 = [sb.tile([P, P * SLOTS], BF16, name="w2_bf16_%d" % t, align_bytes=MX_ALIGN) for t in range(2)]
        w2_bf16_23 = sb.tile([P, 2 * P * SLOTS], BF16, name="w2_bf16_23", align_bytes=MX_ALIGN)
        w1_bf16_01 = sb.tile([P, 2 * P * SLOTS], BF16, name="w1_bf16_01", align_bytes=MX_ALIGN)
        w1_bf16_23 = sb.tile([P, 2 * P * SLOTS], BF16, name="w1_bf16_23", align_bytes=MX_ALIGN)

        for a in range(2):
            quantize(x_codes[:, half(a, S)], x_scales[:, half(a, S)], x_bf16[a][:].rearrange("p c j -> p (c j)"))
        for t in range(2):
            round_tiles01(w2_bf16[t][:], w2_raw[t])
            quantize(w2_codes[:, tile_columns(t)], w2_scales[:, tile_columns(t)], w2_bf16[t][:])
        w2_view23 = w2_bf16_23[:].rearrange("p (s a g b j) -> p a s g j b", s=2, a=2, b=2, j=SLOTS)
        for a in range(2):
            round_tiles23(w2_view23[:, a], w2_raw[a])
        quantize(w2_codes[:, half(1, H)], w2_scales23, w2_bf16_23[:])

        e = [sb.tile([P, S], F32, name=name, align_bytes=MX_ALIGN) for name in ("w2_bf16_1", "e1", "e2", "e3")]
        y = [sb.tile([P, S], F32, name="y%d" % t) for t in range(SLOTS)]

        def first_product(dst, bank, w_codes, w_scales):
            product(dst[:], bank, w_codes, w_scales, x_codes[:], x_scales[:])

        for a in range(2):
            product(e[0][:, half(a, S)], a, w2_codes[:, tile_columns(0)], w2_scales[:, tile_columns(0)],
                    x_codes[:, half(a, S)], x_scales[:, half(a, S)])

        centre = [sb.tile([P, V], F32, name="centre%d" % t) for t in range(2)]
        near0 = [sb.tile([P, V], F32, name="near0_%d" % d)[:] for d in range(NEIGHBOURS)]
        first_product(e[1], 2, w2_codes[:, tile_columns(1)], w2_scales[:, tile_columns(1)])
        for d in range(NEIGHBOURS):
            fetch(near0[d], e[0], pos_list[d][:])
        round_tiles01(w1_bf16_01[:], w1_raw)
        for t in range(2):
            quantize(w1_codes[:, tile_columns(t)], w1_scales[:, tile_columns(t)], w1_bf16_01[:, half(t, 2 * P * SLOTS)])
        reused = w1_bf16_01[:].bitcast(F32)
        near1_own = sb.tile([P, V], F32, name="near1_own")
        near1 = [reused[:, :V], reused[:, V:], near1_own[:]]
        fetch(near1[2], e[1], pos_list[2][:])
        for d in range(2):
            fetch(near1[d], e[1], pos_list[d][:])
        round_tiles23(w1_bf16_23[:].rearrange("p (s g b j) -> p s g j b", s=2, b=2, j=SLOTS), w1_raw)
        quantize(w1_codes[:, half(1, H)], w1_scales[:, half(1, H)], w1_bf16_23[:])
        for t in range(2):
            first_product(y[t], t, w1_codes[:, tile_columns(t)], w1_scales[:, tile_columns(t)])
            fetch(centre[t][:], y[t], cen_list[:])
        for t in (2, 3):
            first_product(e[t], 5 - t, w2_codes[:, tile_columns(t)], w2_scales23[:, tile_columns(t - 2)])

        near2_01 = sb.tile([P, 2 * V], F32, name="near2_01", align_bytes=MX_ALIGN)
        join_left = sb.tile([P, 2 * V], F32, name="join_left")
        join_right = sb.tile([P, 2 * V], F32, name="join_right")
        joined = sb.tile([P, 2 * V], F32, name="joined")
        near3_2 = sb.tile([P, V], F32, name="near3_2")
        largest3 = sb.tile([P, V], F32, name="largest3")
        fetch(near2_01[:, :V], e[2], pos_list[0][:])
        fetch(near2_01[:, V:], e[2], pos_list[1][:])
        fetch(join_right[:, :V], e[2], pos_list[2][:])
        nc.vector.tensor_tensor(join_left[:, :V], near2_01[:, :V], near2_01[:, V:], MAX)

        candidate = []
        for d in range(NEIGHBOURS):
            sums = ps.tile([P, 2, 2, P], F32, name="sums%d" % d)
            for t, near in enumerate((near0, near1)):
                for group in range(2):
                    centres = half(group, V)
                    nc.tensor.matmul(sums[:, group, t, :], centre[t][:, centres], identity[:],
                                     start=True, stop=False, is_transpose=True)
                    nc.tensor.matmul(sums[:, group, t, :], near[d][:, centres], identity[:],
                                     start=False, stop=True, is_transpose=True)
            rounded = sb.tile([P, 2 * P * 2], BF16, name="candidate%d" % d)
            nc.scalar.activation(rounded[:].rearrange("v (x b s) -> v x b s", b=2, s=2),
                                 sums[:].rearrange("v group t (r s b) -> v (group t r) b s", s=2, b=2), RELU)
            candidate.append(rounded)
        for t in (2, 3):
            first_product(y[t], 5 - t, w1_codes[:, tile_columns(t)], w1_scales[:, tile_columns(t)])

        w3_bf16 = sb.tile([P, N, SLOTS], BF16, name="near2_01", align_bytes=MX_ALIGN)
        w3_codes = sb.tile([P, N], U32, name="w3_codes", align_bytes=MX_ALIGN)
        w3_scales = sb.tile([P, N], U8, name="w3_scales", align_bytes=MX_ALIGN)
        nc.scalar.copy(w3_bf16[:], w3_raw[:].rearrange("p t n -> p n t"))

        fetch(join_left[:, V:], e[3], pos_list[0][:])
        fetch(join_right[:, V:], e[3], pos_list[1][:])
        fetch(near3_2[:], e[3], pos_list[2][:])
        larger01 = sb.tile([P, 2 * V], BF16, name="larger01")
        nc.vector.tensor_tensor(larger01[:], candidate[0][:], candidate[1][:], MAX)
        nc.vector.tensor_tensor(joined[:], join_left[:], join_right[:], MAX)
        z_turned = sb.tile([P, 2 * V], BF16, name="z_turned")
        nc.vector.tensor_tensor(z_turned[:], larger01[:], candidate[2][:], MAX)
        nc.vector.tensor_tensor(largest3[:], joined[:, V:], near3_2[:], MAX)
        quantize(w3_codes[:], w3_scales[:], w3_bf16[:].rearrange("p n t -> p (n t)"))

        z_words = ps.tile([P, V], F32, name="z_words")
        for group in range(2):
            nc.tensor.transpose(z_words[:, half(group, V)], z_turned[:].bitcast(F32)[:, half(group, V)], identity[:])
        z_bf16 = [sb.tile([P, V // 2 * SLOTS], BF16, name="z_bf16_%d" % group, align_bytes=MX_ALIGN) for group in range(2)]
        for group in range(2):
            nc.scalar.copy(z_bf16[group][:].bitcast(F32).rearrange("p (v u) -> p v u", u=2)[:, :, 0],
                           z_words[:, half(group, V)])

        largest = [joined[:, :V], largest3[:]]
        summed = [sb.tile([P, 2, V // 2], F32, name="summed%d" % group) for group in range(2)]

        def add_centres(group):
            offsets = cen_list[:, half(group, V // PER_COLUMN)]
            for s in range(2):
                nc.vector.tensor_tensor(summed[group][:, s, :], y[2 + s][:].indirect(offsets),
                                        largest[s][:, half(group, V)], ADD)

        def slots23(group):
            return z_bf16[group][:].rearrange("p (v t) -> p v t", t=SLOTS)[:, :, 2:4]

        def last_product(group):
            z_codes = sb.tile([P, V // 2], U32, name="z_codes%d" % group, align_bytes=MX_ALIGN)
            z_scales = sb.tile([P, V // 2], U8, name="z_scales%d" % group, align_bytes=MX_ALIGN)
            quantize(z_codes[:], z_scales[:], z_bf16[group][:])
            result = sb.tile([P, V // 2], F32, name="result%d" % group)
            product(result[:], group, w3_codes[:], w3_scales[:], z_codes[:], z_scales[:])
            nc.sync.dma_start(out[:, half(group, V)], result[:])

        add_centres(0)
        nc.scalar.activation(slots23(0), summed[0][:].rearrange("p s v -> p v s"), RELU)
        add_centres(1)
        last_product(0)
        nc.vector.tensor_scalar_max(slots23(1), summed[1][:].rearrange("p s v -> p v s"), 0.0)
        last_product(1)
